import numpy as np
CORES = [5,13,21,29,37,45,53,61,69,77,85,93,101,109,117,125,133,141,149,157,165,173,181,189,197,205,213,221,229,237,245,253]
N = 32
ROOT = 31
def setup_inputs(rng):
    return {"x": rng.standard_normal((N, 128, 128), dtype=np.float32)}
def reference(x):
    y = np.full(x.shape, np.nan, x.dtype)
    y[ROOT] = x.sum(axis=0, dtype=np.float64).astype(x.dtype)
    return {"y": y}

@@ -1,0 +1,75 @@
+from concourse.bass import RemoteDMATransfer, DstId
+
+K = 16
+W = 128 // K
+PLANE = 16
+ROOT = 253
+
+SCRATCH = {
+    "xs": ("dram", [K, 128, W], "float32"),
+    "land": ("dram", [PLANE + 1, 128, W], "float32"),
+    "res": ("dram", [K, 128, W], "float32"),
+}
+SEMAPHORES = ["loaded", "sent", "arrived", "done", "stored"]
+
+
+def even_folder(p):
+    return 8 * (2 * p) + 6
+
+
+def odd_folder(p):
+    return 8 * (2 * p + 1) + (6 if p % 2 else 2)
+
+
+def engines(mask):
+    return bin(mask).count("1")
+
+
+def transfer(topo, src, dst, srcs, out, mask, sem):
+    rid, pid = topo.addr(dst, src)
+    return RemoteDMATransfer(dst_ids=[DstId(rid=rid, pnc=pid)], dma_engine_mask=mask, remote_sem=sem,
+                             srcs=srcs, dsts=[out], alu_op=1 if len(srcs) > 1 else 0)
+
+
+def rank_program(g, core, T, topo):
+    sem = T.sem
+    rank = T.rank_of(core)
+    sent = 0
+
+    if rank is not None:
+        parity, i = rank % 2, rank // 2
+        folder = odd_folder if parity else even_folder
+        g.dma_start(T.xs[:], T.x[:]).then_inc(sem.loaded, 16)
+        g.wait_ge(sem.loaded, 16)
+        order = [(i + 1 + t) % K for t in range(K)]
+        for c in range(0, K, 8):
+            g.remote_dma_fused(
+                [transfer(topo, core, folder(p), [T.xs[p]], T.land[i], 1 << e, sem.arrived)
+                 for e, p in enumerate(order[c:c + 8])],
+                local_sem=sem.sent)
+            sent += len(order[c:c + 8])
+
+    for p in range(K):
+        if core == even_folder(p):
+            dst = odd_folder(p)
+            mask = topo.mask(core, dst)
+            g.wait_ge(sem.arrived, PLANE)
+            g.remote_dma_fused(
+                [transfer(topo, core, dst, [T.land[s] for s in range(PLANE)], T.land[PLANE], mask, sem.arrived)],
+                local_sem=sem.sent)
+            sent += engines(mask)
+        if core == odd_folder(p):
+            mask = topo.mask(core, ROOT)
+            g.wait_ge(sem.arrived, PLANE + engines(topo.mask(even_folder(p), core)))
+            g.remote_dma_fused(
+                [transfer(topo, core, ROOT, [T.land[s] for s in range(PLANE + 1)], T.res[p], mask, sem.done)],
+                local_sem=sem.sent)
+            sent += engines(mask)
+
+    if core == ROOT:
+        g.wait_ge(sem.done, sum(engines(topo.mask(odd_folder(p), ROOT)) for p in range(K)))
+        g.dma_start(T.y[:], T.res[:]).then_inc(sem.stored, 16)
+        g.wait_ge(sem.stored, 16)
+
+    if sent:
+        g.wait_ge(sem.sent, sent)

@@ -1,6 +1,9 @@
 from concourse.bass import RemoteDMATransfer, DstId
+from concourse.mybir import AluOpType
 
 K = 16
+ACC = True
+PAIR = [p * (16 // K) + (16 // K - 1) for p in range(K)]
 W = 128 // K
 PLANE = 16
 ROOT = 253
@@ -9,16 +12,17 @@ SCRATCH = {
     "xs": ("dram", [K, 128, W], "float32"),
     "land": ("dram", [PLANE + 1, 128, W], "float32"),
     "res": ("dram", [K, 128, W], "float32"),
+    "res2": ("dram", [K, 128, W], "float32"),
 }
-SEMAPHORES = ["loaded", "sent", "arrived", "done", "stored"]
+SEMAPHORES = ["loaded", "sent", "arrived", "done", "done2", "stored"]
 
 
 def even_folder(p):
-    return 8 * (2 * p) + 6
+    return 8 * (2 * PAIR[p]) + (2 if ACC else 6)
 
 
 def odd_folder(p):
-    return 8 * (2 * p + 1) + (6 if p % 2 else 2)
+    return 8 * (2 * PAIR[p] + 1) + (6 if (ACC or p % 2) else 2)
 
 
 def engines(mask):
@@ -51,18 +55,20 @@ def rank_program(g, core, T, topo):
 
     for p in range(K):
         if core == even_folder(p):
-            dst = odd_folder(p)
+            dst = ROOT if ACC else odd_folder(p)
             mask = topo.mask(core, dst)
             g.wait_ge(sem.arrived, PLANE)
             g.remote_dma_fused(
-                [transfer(topo, core, dst, [T.land[s] for s in range(PLANE)], T.land[PLANE], mask, sem.arrived)],
+                [transfer(topo, core, dst, [T.land[s] for s in range(PLANE)],
+                          T.res2[p] if ACC else T.land[PLANE], mask, sem.done2 if ACC else sem.arrived)],
                 local_sem=sem.sent)
             sent += engines(mask)
         if core == odd_folder(p):
             mask = topo.mask(core, ROOT)
-            g.wait_ge(sem.arrived, PLANE + engines(topo.mask(even_folder(p), core)))
+            n = PLANE if ACC else PLANE + 1
+            g.wait_ge(sem.arrived, PLANE + (0 if ACC else engines(topo.mask(even_folder(p), core))))
             g.remote_dma_fused(
-                [transfer(topo, core, ROOT, [T.land[s] for s in range(PLANE + 1)], T.res[p], mask, sem.done)],
+                [transfer(topo, core, ROOT, [T.land[s] for s in range(n)], T.res[p], mask, sem.done)],
                 local_sem=sem.sent)
             sent += engines(mask)
 
@@ -70,6 +76,10 @@ def rank_program(g, core, T, topo):
         g.wait_ge(sem.done, sum(engines(topo.mask(odd_folder(p), ROOT)) for p in range(K)))
         g.dma_start(T.y[:], T.res[:]).then_inc(sem.stored, 16)
         g.wait_ge(sem.stored, 16)
+        if ACC:
+            g.wait_ge(sem.done2, sum(engines(topo.mask(even_folder(p), ROOT)) for p in range(K)))
+            g.dma_start(T.y[:], T.res2[:], accum_op=AluOpType.add, max_dma_last_dim=8192).then_inc(sem.stored, 16)
+            g.wait_ge(sem.stored, 32)
 
     if sent:
         g.wait_ge(sem.sent, sent)

@@ -2,15 +2,13 @@ from concourse.bass import RemoteDMATransfer, DstId
 from concourse.mybir import AluOpType
 
 K = 16
-ACC = True
-PAIR = [p * (16 // K) + (16 // K - 1) for p in range(K)]
 W = 128 // K
 PLANE = 16
 ROOT = 253
 
 SCRATCH = {
     "xs": ("dram", [K, 128, W], "float32"),
-    "land": ("dram", [PLANE + 1, 128, W], "float32"),
+    "land": ("dram", [PLANE, 128, W], "float32"),
     "res": ("dram", [K, 128, W], "float32"),
     "res2": ("dram", [K, 128, W], "float32"),
 }
@@ -18,11 +16,11 @@ SEMAPHORES = ["loaded", "sent", "arrived", "done", "done2", "stored"]
 
 
 def even_folder(p):
-    return 8 * (2 * PAIR[p]) + (2 if ACC else 6)
+    return 8 * (2 * p) + 2
 
 
 def odd_folder(p):
-    return 8 * (2 * PAIR[p] + 1) + (6 if (ACC or p % 2) else 2)
+    return 8 * (2 * p + 1) + 6
 
 
 def engines(mask):
@@ -51,35 +49,25 @@ def rank_program(g, core, T, topo):
                 [transfer(topo, core, folder(p), [T.xs[p]], T.land[i], 1 << e, sem.arrived)
                  for e, p in enumerate(order[c:c + 8])],
                 local_sem=sem.sent)
-            sent += len(order[c:c + 8])
+            sent += 8
 
     for p in range(K):
-        if core == even_folder(p):
-            dst = ROOT if ACC else odd_folder(p)
-            mask = topo.mask(core, dst)
-            g.wait_ge(sem.arrived, PLANE)
-            g.remote_dma_fused(
-                [transfer(topo, core, dst, [T.land[s] for s in range(PLANE)],
-                          T.res2[p] if ACC else T.land[PLANE], mask, sem.done2 if ACC else sem.arrived)],
-                local_sem=sem.sent)
-            sent += engines(mask)
-        if core == odd_folder(p):
-            mask = topo.mask(core, ROOT)
-            n = PLANE if ACC else PLANE + 1
-            g.wait_ge(sem.arrived, PLANE + (0 if ACC else engines(topo.mask(even_folder(p), core))))
-            g.remote_dma_fused(
-                [transfer(topo, core, ROOT, [T.land[s] for s in range(n)], T.res[p], mask, sem.done)],
-                local_sem=sem.sent)
-            sent += engines(mask)
+        for f, out, s in ((even_folder(p), T.res2[p], sem.done2), (odd_folder(p), T.res[p], sem.done)):
+            if core == f:
+                mask = topo.mask(core, ROOT)
+                g.wait_ge(sem.arrived, PLANE)
+                g.remote_dma_fused(
+                    [transfer(topo, core, ROOT, [T.land[r] for r in range(PLANE)], out, mask, s)],
+                    local_sem=sem.sent)
+                sent += engines(mask)
 
     if core == ROOT:
         g.wait_ge(sem.done, sum(engines(topo.mask(odd_folder(p), ROOT)) for p in range(K)))
         g.dma_start(T.y[:], T.res[:]).then_inc(sem.stored, 16)
         g.wait_ge(sem.stored, 16)
-        if ACC:
-            g.wait_ge(sem.done2, sum(engines(topo.mask(even_folder(p), ROOT)) for p in range(K)))
-            g.dma_start(T.y[:], T.res2[:], accum_op=AluOpType.add, max_dma_last_dim=8192).then_inc(sem.stored, 16)
-            g.wait_ge(sem.stored, 32)
+        g.wait_ge(sem.done2, sum(engines(topo.mask(even_folder(p), ROOT)) for p in range(K)))
+        g.dma_start(T.y[:], T.res2[:], accum_op=AluOpType.add, max_dma_last_dim=8192).then_inc(sem.stored, 16)
+        g.wait_ge(sem.stored, 32)
 
     if sent:
         g.wait_ge(sem.sent, sent)

from concourse.bass import RemoteDMATransfer, DstId
from concourse.mybir import AluOpType

K = 16
W = 128 // K
PLANE = 16
ROOT = 253

SCRATCH = {
    "xs": ("dram", [K, 128, W], "float32"),
    "land": ("dram", [PLANE, 128, W], "float32"),
    "res": ("dram", [K, 128, W], "float32"),
    "res2": ("dram", [K, 128, W], "float32"),
}
SEMAPHORES = ["loaded", "sent", "arrived", "done", "done2", "stored"]


def even_folder(p):
    return 8 * (2 * p) + 2


def odd_folder(p):
    return 8 * (2 * p + 1) + 6


def engines(mask):
    return bin(mask).count("1")


def transfer(topo, src, dst, srcs, out, mask, sem):
    rid, pid = topo.addr(dst, src)
    return RemoteDMATransfer(dst_ids=[DstId(rid=rid, pnc=pid)], dma_engine_mask=mask, remote_sem=sem,
                             srcs=srcs, dsts=[out], alu_op=1 if len(srcs) > 1 else 0)


def rank_program(g, core, T, topo):
    sem = T.sem
    rank = T.rank_of(core)
    sent = 0

    if rank is not None:
        parity, i = rank % 2, rank // 2
        folder = odd_folder if parity else even_folder
        g.dma_start(T.xs[:], T.x[:]).then_inc(sem.loaded, 16)
        g.wait_ge(sem.loaded, 16)
        order = [(i + 1 + t) % K for t in range(K)]
        for c in range(0, K, 8):
            g.remote_dma_fused(
                [transfer(topo, core, folder(p), [T.xs[p]], T.land[i], 1 << e, sem.arrived)
                 for e, p in enumerate(order[c:c + 8])],
                local_sem=sem.sent)
            sent += 8

    for p in range(K):
        for f, out, s in ((even_folder(p), T.res2[p], sem.done2), (odd_folder(p), T.res[p], sem.done)):
            if core == f:
                mask = topo.mask(core, ROOT)
                g.wait_ge(sem.arrived, PLANE)
                g.remote_dma_fused(
                    [transfer(topo, core, ROOT, [T.land[r] for r in range(PLANE)], out, mask, s)],
                    local_sem=sem.sent)
                sent += engines(mask)

    if core == ROOT:
        g.wait_ge(sem.done, sum(engines(topo.mask(odd_folder(p), ROOT)) for p in range(K)))
        g.dma_start(T.y[:], T.res[:]).then_inc(sem.stored, 16)
        g.wait_ge(sem.stored, 16)
        g.wait_ge(sem.done2, sum(engines(topo.mask(even_folder(p), ROOT)) for p in range(K)))
        g.dma_start(T.y[:], T.res2[:], accum_op=AluOpType.add, max_dma_last_dim=8192).then_inc(sem.stored, 16)
        g.wait_ge(sem.stored, 32)

    if sent:
        g.wait_ge(sem.sent, sent)
